import numpy as np
import ml_dtypes


def mxq(x, axis, fmt="e4m3"):
    dtype, down = {"e4m3": (ml_dtypes.float8_e4m3fn, 7), "e5m2": (ml_dtypes.float8_e5m2, 14)}[fmt]
    v = np.moveaxis(np.asarray(x, np.float32).astype(ml_dtypes.bfloat16).astype(np.float64), axis, -1)
    blocks = v.reshape(v.shape[:-1] + (-1, 32))
    amax = np.abs(blocks).max(-1, keepdims=True)
    byte = np.maximum(np.where(amax > 0, np.frexp(amax)[1] - 1 + 127, 0) - down, 1)
    scale = np.exp2(byte - 127.0)
    codes = (blocks / scale).astype(np.float32).astype(dtype).astype(np.float64)
    return np.moveaxis((codes * scale).reshape(v.shape), -1, axis)


WIDE = False


def mx_kscale(k):
    if not WIDE:
        return np.ones(k)
    levels = np.array([30, -30])
    if k % 512:
        return np.exp2(np.random.permutation(np.resize(levels, k // 32))).repeat(32)
    a = np.empty((k // 512, 16))
    for p in range(k // 512):
        a[p, :8] = np.random.permutation(np.resize(levels, 8))
        for g in range(8):
            far = levels[np.abs(levels - a[p, g]) >= 10]
            a[p, g + 8] = far[np.random.randint(len(far))]
    return np.exp2(a.ravel()).repeat(32)


def f64(x):
    return np.asarray(x).astype(np.float64)


def striped(idx):
    return np.tile(np.asarray(idx).reshape(-1, 16).T, (8, 1)).astype(np.uint16)


def unstriped(offs):
    return offs[:16].T.reshape(-1).astype(np.int64)


def bf(x):
    return np.asarray(x, np.float32).astype(ml_dtypes.bfloat16)


def planes(Y):
    r, m = Y.shape
    b = f64(bf(Y)).reshape(r // 32, 32, m)
    amax = np.abs(b).max(1)
    byte = np.clip(np.where(amax > 0, np.frexp(amax)[1] - 1 + 127 - 7, 1), 1, 254)
    codes = (b * np.exp2(127.0 - byte)[:, None, :]).reshape(r, m).astype(np.float32).astype(ml_dtypes.float8_e4m3fn).view(np.uint8)
    words = codes.reshape(r // 512, 128, 4, m).transpose(0, 1, 3, 2)
    return np.ascontiguousarray(words), np.ascontiguousarray(byte.astype(np.uint8).reshape(r // 512, 16, m))


K, J, N, T, V = 512, 512, 256, 1024, 1024


def setup_inputs():
    n = np.random.standard_normal
    idx = np.random.permutation(T)[:J]
    idx2 = np.random.permutation(T)[:J]
    idx3 = np.random.permutation(V)[:J]
    idx4 = np.random.permutation(V)[:J]
    fj = mx_kscale(J)
    return {
        "xf": (n((K, T))).astype(np.float32),
        "ra": (np.random.uniform(0.5, 1.5, (1, J)) * fj).astype(np.float32),
        "gt": (n((N, V)) * np.exp(0.5 * n((1, V)))).astype(np.float32),
        "rb": (np.random.uniform(0.5, 1.5, (1, J)) / fj).astype(np.float32),
        "bn": (np.random.uniform(-0.5, 0.5, (1, N))).astype(np.float32),
        "offs": striped(idx),
        "offs2": striped(idx2),
        "offs3": striped(idx3),
        "offs4": striped(idx4),
    }


def reference(xf, ra, gt, rb, bn, offs, offs2, offs3, offs4):
    idx = unstriped(offs)
    idx2 = unstriped(offs2)
    idx3 = unstriped(offs3)
    idx4 = unstriped(offs4)
    us = np.maximum(f64(xf)[:, idx], f64(xf)[:, idx2]) * f64(ra)
    uj = us.T
    gs = (f64(gt)[:, idx3] - 0.7 * f64(gt)[:, idx4]) * f64(rb)
    gj = gs.T
    ujq = mxq(uj, 0, "e5m2")
    gjq = mxq(gj, 0, "e5m2")
    w = ujq.T @ gjq
    ew = np.exp(0.02 * w + f64(bn))
    y = 256.0 * ew / np.sum(ew, axis=1, keepdims=True)
    words, scales = planes(y)
    return y, words, scales

@@ -1,0 +1,154 @@
+from contextlib import ExitStack
+
+import concourse.mybir as mybir
+from concourse.masks import make_identity
+
+K, J, N, T = 512, 512, 256, 1024
+FLOPS = 2 * K * J * N
+
+F32 = mybir.dt.float32
+BF16 = mybir.dt.bfloat16
+I32 = mybir.dt.int32
+U32 = mybir.dt.uint32
+U16 = mybir.dt.uint16
+U8 = mybir.dt.uint8
+E5M2X4 = mybir.dt.float8_e5m2_x4
+E4M3X4 = mybir.dt.float8_e4m3fn_x4
+ALU = mybir.AluOpType
+ACT = mybir.ActivationFunctionType
+
+P = 128
+PACK = 4
+RUN = 8
+
+
+def tile_list_moment_larger_differences_shares_pl_kernel(
+    tc, xf, ra, gt, rb, bn, offs, offs2, offs3, offs4, out_0, out_1, out_2
+):
+    nc = tc.nc
+    with ExitStack() as ctx:
+        keep = ctx.enter_context(tc.tile_pool(name="keep", bufs=1))
+        psum = ctx.enter_context(tc.psum_pool(name="psum", bufs=1))
+
+        lists = [keep.tile([P, J // 16], U16, name=f"list{i}") for i in range(4)]
+        g_rows = [keep.tile([P, T], F32, name=f"g_rows{h}") for h in range(N // P)]
+        x_rows = [keep.tile([P, T], F32, name=f"x_rows{t}") for t in range(PACK)]
+        xf_dealt = xf.rearrange("(p t) c -> t p c", t=PACK)
+
+        nc.scalar.dma_start(g_rows[0][:], gt[0:P, :])
+        nc.sync.dma_start(lists[2][:], offs3)
+        nc.sync.dma_start(lists[3][:], offs4)
+        nc.sync.dma_start(g_rows[1][:], gt[P : 2 * P, :])
+        nc.sync.dma_start(lists[0][:], offs)
+        nc.sync.dma_start(lists[1][:], offs2)
+        for t in range(PACK):
+            nc.sync.dma_start(x_rows[t][:], xf_dealt[t])
+        bias = keep.tile([P, N], F32)
+        nc.sync.dma_start(bias[:], bn[0].partition_broadcast(P))
+
+        ident = keep.tile([P, P], F32)
+        weight_rows = keep.tile([P, P], F32)
+        nc.gpsimd.memset(weight_rows[:], 0.0)
+        zero = keep.tile([P, 1], F32)
+        nc.vector.memset(zero[:], 0.0)
+        for i, vec in enumerate((ra, rb)):
+            nc.scalar.dma_start(
+                weight_rows[PACK * i : PACK * (i + 1), :].rearrange("s (b r) -> s b r", r=RUN),
+                vec[0].rearrange("(b s r) -> s b r", s=PACK, r=RUN),
+            )
+        nc.scalar.activation(ident[:], zero[:].to_broadcast([P, P]), ACT.Copy)
+        make_identity(nc, ident[:], nomemset=True)
+        weight_bank = psum.tile([P, P], F32)
+        nc.tensor.transpose(weight_bank[:], weight_rows[:], ident[:])
+        weights = keep.tile([P, 2 * PACK], F32)
+        nc.vector.tensor_copy(weights[:], weight_bank[:, 0 : 2 * PACK])
+
+        def gather(on_vector, rows, lst, name, scale=1.0):
+            got = keep.tile([P, J], F32, name=name)
+            if on_vector:
+                nc.vector.tensor_copy(got[:], rows[:].indirect(lst[:]))
+            else:
+                nc.scalar.activation(got[:], rows[:].indirect(lst[:]), ACT.Copy, scale=scale)
+            return got
+
+        def combine(a, b, op, name, pieces=1):
+            both = keep.tile([P, PACK, J // (PACK * RUN), RUN], F32, name=name)
+            view = "p (b s r) -> p s b r"
+            a_view, b_view = a[:].rearrange(view, s=PACK, r=RUN), b[:].rearrange(view, s=PACK, r=RUN)
+            for i in range(pieces):
+                part = slice(i * PACK // pieces, (i + 1) * PACK // pieces)
+                nc.vector.tensor_tensor(both[:, part], a_view[:, part], b_view[:, part], op)
+            bank = psum.tile([P, PACK, P], F32, name="turned", bufs=3)
+            flat = both[:].rearrange("p s b r -> p s (b r)")
+            for s in range(PACK):
+                nc.tensor.transpose(bank[:, s, :], flat[:, s, :], ident[:])
+            return bank
+
+        def weigh(bank, w, dst):
+            nc.vector.tensor_tensor(
+                dst, bank[:].rearrange("p s c -> p c s"), w.unsqueeze(1).to_broadcast([P, P, PACK]), ALU.mult
+            )
+
+        g_in = keep.tile([P, N, PACK], BF16, align_bytes=64)
+        g_codes = keep.tile([P, N], U32, align_bytes=64)
+        g_scales = keep.tile([P, N], U8, align_bytes=64)
+        for h in range(N // P):
+            a = gather(True, g_rows[h], lists[2], f"g_a{h}")
+            b = gather(False, g_rows[h], lists[3], f"g_b{h}", scale=-0.7)
+            bank = combine(a, b, ALU.add, f"g_both{h}")
+            weigh(bank, weights[:, PACK : 2 * PACK], g_in[:, h * P : (h + 1) * P, :])
+        nc.vector.quantize_mx(g_codes[:].bitcast(E5M2X4), g_scales[:], g_in[:].rearrange("p n s -> p (n s)"))
+
+        y = keep.tile([P, PACK, N], F32)
+        out_dealt = out_0.rearrange("(p t) n -> t p n", t=PACK)
+        on_vector = (True, False, False, False)
+        moments = []
+        for t in range(PACK):
+            a = gather(on_vector[t], x_rows[t], lists[0], f"x_a{t}")
+            b = gather(False, x_rows[t], lists[1], f"x_b{t}")
+            bank = combine(a, b, ALU.max, f"x_both{t}", 2 if t == PACK - 1 else 1)
+            u_in = keep.tile([P, P, PACK], BF16, align_bytes=64, name=f"u_in{t}")
+            weigh(bank, weights[:, 0:PACK], u_in[:])
+            u_codes = keep.tile([P, P], U32, align_bytes=64, name=f"u_codes{t}")
+            u_scales = keep.tile([P, P], U8, align_bytes=64, name=f"u_scales{t}")
+            nc.vector.quantize_mx(u_codes[:].bitcast(E5M2X4), u_scales[:], u_in[:].rearrange("p c s -> p (c s)"))
+            w = psum.tile([P, N], F32, name=f"moment{t}")
+            nc.tensor.matmul_mx(
+                w[:],
+                lhsT=u_codes[:].bitcast(E5M2X4),
+                lhsT_scale=u_scales[:],
+                rhs=g_codes[:].bitcast(E5M2X4),
+                rhs_scale=g_scales[:],
+                start=True,
+                stop=True,
+            )
+            moments.append(w)
+
+        y_in = keep.tile([P, N, PACK], BF16, align_bytes=64)
+        z = keep.tile([P, PACK, N], F32, name=f"x_rows{PACK - 1}")
+        for t in range(PACK):
+            nc.vector.scalar_tensor_tensor(z[:, t, :], moments[t][:], 0.02, bias[:], ALU.mult, ALU.add)
+            neg_max = keep.tile([P, 1], F32, name=f"neg_max{t}")
+            nc.vector.tensor_reduce(neg_max[:], z[:, t, :], mybir.AxisListType.X, ALU.max, negate=True)
+            e = keep.tile([P, N], F32, name=f"e{t}")
+            total = keep.tile([P, 1], F32, name=f"total{t}")
+            nc.scalar.activation(e[:], z[:, t, :], ACT.Exp, bias=neg_max[:], accum_out=total[:])
+            inv = keep.tile([P, 1], F32, name=f"inv{t}")
+            nc.vector.reciprocal(inv[:], total[:])
+            if t == PACK - 1:
+                nc.vector.tensor_scalar(y_in[:, :, t], e[:], inv[:], 256.0, ALU.mult, ALU.mult)
+            nc.vector.tensor_scalar(y[:, t, :], e[:], inv[:], 256.0, ALU.mult, ALU.mult)
+            nc.sync.dma_start(out_dealt[t], y[:, t, :])
+            if t == PACK - 2:
+                nc.vector.tensor_copy(
+                    y_in[:, :, 0:3].rearrange("p (c i) t -> p c t i", i=4),
+                    y[:, 0:3, :].rearrange("p t (c i) -> p c t i", i=4),
+                )
+
+        y_codes = keep.tile([P, N], U32, align_bytes=64)
+        y_scales = keep.tile([P, N], U8, align_bytes=64)
+        nc.vector.quantize_mx(y_codes[:].bitcast(E4M3X4), y_scales[:], y_in[:].rearrange("p n t -> p (n t)"))
+        nc.sync.dma_start(out_1[0].rearrange("p c r -> p (c r)").bitcast(I32), y_codes[:].bitcast(I32))
+        for q in range(4):
+            eng = nc.scalar if q % 2 else nc.sync
+            eng.dma_start(out_2[0, 4 * q : 4 * q + 4, :].bitcast(I32), y_scales[32 * q : 32 * q + 4, :].bitcast(I32))

@@ -35,7 +35,7 @@ def tile_list_moment_larger_differences_shares_pl_kernel(
         x_rows = [keep.tile([P, T], F32, name=f"x_rows{t}") for t in range(PACK)]
         xf_dealt = xf.rearrange("(p t) c -> t p c", t=PACK)
 
-        nc.scalar.dma_start(g_rows[0][:], gt[0:P, :])
+        nc.sync.dma_start(g_rows[0][:], gt[0:P, :])
         nc.sync.dma_start(lists[2][:], offs3)
         nc.sync.dma_start(lists[3][:], offs4)
         nc.sync.dma_start(g_rows[1][:], gt[P : 2 * P, :])
@@ -71,13 +71,13 @@ def tile_list_moment_larger_differences_shares_pl_kernel(
                 nc.scalar.activation(got[:], rows[:].indirect(lst[:]), ACT.Copy, scale=scale)
             return got
 
-        def combine(a, b, op, name, pieces=1):
+        def combine(engine, a, b, op, name, pieces=1):
             both = keep.tile([P, PACK, J // (PACK * RUN), RUN], F32, name=name)
             view = "p (b s r) -> p s b r"
             a_view, b_view = a[:].rearrange(view, s=PACK, r=RUN), b[:].rearrange(view, s=PACK, r=RUN)
             for i in range(pieces):
                 part = slice(i * PACK // pieces, (i + 1) * PACK // pieces)
-                nc.vector.tensor_tensor(both[:, part], a_view[:, part], b_view[:, part], op)
+                engine.tensor_tensor(both[:, part], a_view[:, part], b_view[:, part], op)
             bank = psum.tile([P, PACK, P], F32, name="turned", bufs=3)
             flat = both[:].rearrange("p s b r -> p s (b r)")
             for s in range(PACK):
@@ -95,18 +95,18 @@ def tile_list_moment_larger_differences_shares_pl_kernel(
         for h in range(N // P):
             a = gather(True, g_rows[h], lists[2], f"g_a{h}")
             b = gather(False, g_rows[h], lists[3], f"g_b{h}", scale=-0.7)
-            bank = combine(a, b, ALU.add, f"g_both{h}")
+            bank = combine(nc.gpsimd, a, b, ALU.add, f"g_both{h}")
             weigh(bank, weights[:, PACK : 2 * PACK], g_in[:, h * P : (h + 1) * P, :])
         nc.vector.quantize_mx(g_codes[:].bitcast(E5M2X4), g_scales[:], g_in[:].rearrange("p n s -> p (n s)"))
 
         y = keep.tile([P, PACK, N], F32)
         out_dealt = out_0.rearrange("(p t) n -> t p n", t=PACK)
-        on_vector = (True, False, False, False)
+        on_vector = (True, True, False, False)
         moments = []
         for t in range(PACK):
             a = gather(on_vector[t], x_rows[t], lists[0], f"x_a{t}")
             b = gather(False, x_rows[t], lists[1], f"x_b{t}")
-            bank = combine(a, b, ALU.max, f"x_both{t}", 2 if t == PACK - 1 else 1)
+            bank = combine(nc.vector, a, b, ALU.max, f"x_both{t}", 2 if t == PACK - 1 else 1)
             u_in = keep.tile([P, P, PACK], BF16, align_bytes=64, name=f"u_in{t}")
             weigh(bank, weights[:, 0:PACK], u_in[:])
             u_codes = keep.tile([P, P], U32, align_bytes=64, name=f"u_codes{t}")

from contextlib import ExitStack

import concourse.mybir as mybir
from concourse.masks import make_identity

K, J, N, T = 512, 512, 256, 1024
FLOPS = 2 * K * J * N

F32 = mybir.dt.float32
BF16 = mybir.dt.bfloat16
I32 = mybir.dt.int32
U32 = mybir.dt.uint32
U16 = mybir.dt.uint16
U8 = mybir.dt.uint8
E5M2X4 = mybir.dt.float8_e5m2_x4
E4M3X4 = mybir.dt.float8_e4m3fn_x4
ALU = mybir.AluOpType
ACT = mybir.ActivationFunctionType

P = 128
PACK = 4
RUN = 8


def tile_list_moment_larger_differences_shares_pl_kernel(
    tc, xf, ra, gt, rb, bn, offs, offs2, offs3, offs4, out_0, out_1, out_2
):
    nc = tc.nc
    with ExitStack() as ctx:
        keep = ctx.enter_context(tc.tile_pool(name="keep", bufs=1))
        psum = ctx.enter_context(tc.psum_pool(name="psum", bufs=1))

        lists = [keep.tile([P, J // 16], U16, name=f"list{i}") for i in range(4)]
        g_rows = [keep.tile([P, T], F32, name=f"g_rows{h}") for h in range(N // P)]
        x_rows = [keep.tile([P, T], F32, name=f"x_rows{t}") for t in range(PACK)]
        xf_dealt = xf.rearrange("(p t) c -> t p c", t=PACK)

        nc.sync.dma_start(g_rows[0][:], gt[0:P, :])
        nc.sync.dma_start(lists[2][:], offs3)
        nc.sync.dma_start(lists[3][:], offs4)
        nc.sync.dma_start(g_rows[1][:], gt[P : 2 * P, :])
        nc.sync.dma_start(lists[0][:], offs)
        nc.sync.dma_start(lists[1][:], offs2)
        for t in range(PACK):
            nc.sync.dma_start(x_rows[t][:], xf_dealt[t])
        bias = keep.tile([P, N], F32)
        nc.sync.dma_start(bias[:], bn[0].partition_broadcast(P))

        ident = keep.tile([P, P], F32)
        weight_rows = keep.tile([P, P], F32)
        nc.gpsimd.memset(weight_rows[:], 0.0)
        zero = keep.tile([P, 1], F32)
        nc.vector.memset(zero[:], 0.0)
        for i, vec in enumerate((ra, rb)):
            nc.scalar.dma_start(
                weight_rows[PACK * i : PACK * (i + 1), :].rearrange("s (b r) -> s b r", r=RUN),
                vec[0].rearrange("(b s r) -> s b r", s=PACK, r=RUN),
            )
        nc.scalar.activation(ident[:], zero[:].to_broadcast([P, P]), ACT.Copy)
        make_identity(nc, ident[:], nomemset=True)
        weight_bank = psum.tile([P, P], F32)
        nc.tensor.transpose(weight_bank[:], weight_rows[:], ident[:])
        weights = keep.tile([P, 2 * PACK], F32)
        nc.vector.tensor_copy(weights[:], weight_bank[:, 0 : 2 * PACK])

        def gather(on_vector, rows, lst, name, scale=1.0):
            got = keep.tile([P, J], F32, name=name)
            if on_vector:
                nc.vector.tensor_copy(got[:], rows[:].indirect(lst[:]))
            else:
                nc.scalar.activation(got[:], rows[:].indirect(lst[:]), ACT.Copy, scale=scale)
            return got

        def combine(engine, a, b, op, name, pieces=1):
            both = keep.tile([P, PACK, J // (PACK * RUN), RUN], F32, name=name)
            view = "p (b s r) -> p s b r"
            a_view, b_view = a[:].rearrange(view, s=PACK, r=RUN), b[:].rearrange(view, s=PACK, r=RUN)
            for i in range(pieces):
                part = slice(i * PACK // pieces, (i + 1) * PACK // pieces)
                engine.tensor_tensor(both[:, part], a_view[:, part], b_view[:, part], op)
            bank = psum.tile([P, PACK, P], F32, name="turned", bufs=3)
            flat = both[:].rearrange("p s b r -> p s (b r)")
            for s in range(PACK):
                nc.tensor.transpose(bank[:, s, :], flat[:, s, :], ident[:])
            return bank

        def weigh(bank, w, dst):
            nc.vector.tensor_tensor(
                dst, bank[:].rearrange("p s c -> p c s"), w.unsqueeze(1).to_broadcast([P, P, PACK]), ALU.mult
            )

        g_in = keep.tile([P, N, PACK], BF16, align_bytes=64)
        g_codes = keep.tile([P, N], U32, align_bytes=64)
        g_scales = keep.tile([P, N], U8, align_bytes=64)
        for h in range(N // P):
            a = gather(True, g_rows[h], lists[2], f"g_a{h}")
            b = gather(False, g_rows[h], lists[3], f"g_b{h}", scale=-0.7)
            bank = combine(nc.gpsimd, a, b, ALU.add, f"g_both{h}")
            weigh(bank, weights[:, PACK : 2 * PACK], g_in[:, h * P : (h + 1) * P, :])
        nc.vector.quantize_mx(g_codes[:].bitcast(E5M2X4), g_scales[:], g_in[:].rearrange("p n s -> p (n s)"))

        y = keep.tile([P, PACK, N], F32)
        out_dealt = out_0.rearrange("(p t) n -> t p n", t=PACK)
        on_vector = (True, True, False, False)
        moments = []
        for t in range(PACK):
            a = gather(on_vector[t], x_rows[t], lists[0], f"x_a{t}")
            b = gather(False, x_rows[t], lists[1], f"x_b{t}")
            bank = combine(nc.vector, a, b, ALU.max, f"x_both{t}", 2 if t == PACK - 1 else 1)
            u_in = keep.tile([P, P, PACK], BF16, align_bytes=64, name=f"u_in{t}")
            weigh(bank, weights[:, 0:PACK], u_in[:])
            u_codes = keep.tile([P, P], U32, align_bytes=64, name=f"u_codes{t}")
            u_scales = keep.tile([P, P], U8, align_bytes=64, name=f"u_scales{t}")
            nc.vector.quantize_mx(u_codes[:].bitcast(E5M2X4), u_scales[:], u_in[:].rearrange("p c s -> p (c s)"))
            w = psum.tile([P, N], F32, name=f"moment{t}")
            nc.tensor.matmul_mx(
                w[:],
                lhsT=u_codes[:].bitcast(E5M2X4),
                lhsT_scale=u_scales[:],
                rhs=g_codes[:].bitcast(E5M2X4),
                rhs_scale=g_scales[:],
                start=True,
                stop=True,
            )
            moments.append(w)

        y_in = keep.tile([P, N, PACK], BF16, align_bytes=64)
        z = keep.tile([P, PACK, N], F32, name=f"x_rows{PACK - 1}")
        for t in range(PACK):
            nc.vector.scalar_tensor_tensor(z[:, t, :], moments[t][:], 0.02, bias[:], ALU.mult, ALU.add)
            neg_max = keep.tile([P, 1], F32, name=f"neg_max{t}")
            nc.vector.tensor_reduce(neg_max[:], z[:, t, :], mybir.AxisListType.X, ALU.max, negate=True)
            e = keep.tile([P, N], F32, name=f"e{t}")
            total = keep.tile([P, 1], F32, name=f"total{t}")
            nc.scalar.activation(e[:], z[:, t, :], ACT.Exp, bias=neg_max[:], accum_out=total[:])
            inv = keep.tile([P, 1], F32, name=f"inv{t}")
            nc.vector.reciprocal(inv[:], total[:])
            if t == PACK - 1:
                nc.vector.tensor_scalar(y_in[:, :, t], e[:], inv[:], 256.0, ALU.mult, ALU.mult)
            nc.vector.tensor_scalar(y[:, t, :], e[:], inv[:], 256.0, ALU.mult, ALU.mult)
            nc.sync.dma_start(out_dealt[t], y[:, t, :])
            if t == PACK - 2:
                nc.vector.tensor_copy(
                    y_in[:, :, 0:3].rearrange("p (c i) t -> p c t i", i=4),
                    y[:, 0:3, :].rearrange("p t (c i) -> p c t i", i=4),
                )

        y_codes = keep.tile([P, N], U32, align_bytes=64)
        y_scales = keep.tile([P, N], U8, align_bytes=64)
        nc.vector.quantize_mx(y_codes[:].bitcast(E4M3X4), y_scales[:], y_in[:].rearrange("p n t -> p (n t)"))
        nc.sync.dma_start(out_1[0].rearrange("p c r -> p (c r)").bitcast(I32), y_codes[:].bitcast(I32))
        for q in range(4):
            eng = nc.scalar if q % 2 else nc.sync
            eng.dma_start(out_2[0, 4 * q : 4 * q + 4, :].bitcast(I32), y_scales[32 * q : 32 * q + 4, :].bitcast(I32))
